import numpy as np
import ml_dtypes


def mxq(x, axis, fmt="e4m3"):
    dtype, down = {"e4m3": (ml_dtypes.float8_e4m3fn, 7), "e5m2": (ml_dtypes.float8_e5m2, 14)}[fmt]
    v = np.moveaxis(np.asarray(x, np.float32).astype(ml_dtypes.bfloat16).astype(np.float64), axis, -1)
    blocks = v.reshape(v.shape[:-1] + (-1, 32))
    amax = np.abs(blocks).max(-1, keepdims=True)
    byte = np.maximum(np.where(amax > 0, np.frexp(amax)[1] - 1 + 127, 0) - down, 1)
    scale = np.exp2(byte - 127.0)
    codes = (blocks / scale).astype(np.float32).astype(dtype).astype(np.float64)
    return np.moveaxis((codes * scale).reshape(v.shape), -1, axis)


WIDE = False


def mx_kscale(k, group=512):
    if not WIDE:
        return np.ones(k)
    levels = np.array([10, -10, 5, -5, 0])
    if group != 512:
        return np.exp2(np.random.permutation(np.resize(levels, k // group))).repeat(group)
    if k % 512:
        return np.exp2(np.random.permutation(np.resize(levels, k // 32))).repeat(32)
    a = np.empty((k // 512, 16))
    for p in range(k // 512):
        a[p, :8] = np.random.permutation(np.resize(levels, 8))
        for g in range(8):
            far = levels[np.abs(levels - a[p, g]) >= 10]
            a[p, g + 8] = far[np.random.randint(len(far))]
    return np.exp2(a.ravel()).repeat(32)


def f64(x):
    return np.asarray(x).astype(np.float64)


def striped(idx):
    return np.tile(np.asarray(idx).reshape(-1, 16).T, (8, 1)).astype(np.uint16)


def unstriped(offs):
    return offs[:16].T.reshape(-1).astype(np.int64)


H, KV, D, NQ, N = 4, 1, 128, 512, 512


def setup_inputs():
    n = np.random.standard_normal
    s = mx_kscale(D, 0)[:, None]
    u = mx_kscale(N)
    t = np.random.uniform(0.5, 2.0, N) * u
    v = n((KV, N, 128))
    return {
        "qT": (n((H, D, NQ)) * s * (0.70 / np.sqrt(D))).astype(np.float32),
        "kT": (n((KV, D, N)) / s).astype(np.float32),
        "t": t.reshape(N, 1).astype(np.float32),
        "v": (v / t[:, None]).astype(np.float32),
        "kb": (0.5 * n((N, 1))).astype(np.float32),
        "mask": (np.arange(N)[:, None] <= np.sort(np.random.randint(N // 4, N, NQ))[None, :]).astype(np.float32),
        "og": n((H, NQ, 128)).astype(np.float32),
    }


def reference(qT, kT, t, v, kb, mask, og):
    a = np.repeat(mxq(f64(kT), 1, "e4m3"), H // KV, 0).transpose(0, 2, 1) @ mxq(f64(qT), 1, "e4m3")
    a = a + f64(kb)
    p = np.maximum(a, 0.0)
    p = p * f64(mask)
    w = p * f64(t)
    y = mxq(w, 1, "e4m3").transpose(0, 2, 1) @ np.repeat(mxq(f64(v), 1, "e4m3"), H // KV, 0)
    y = y / 16.0
    y = y / (1.0 + np.exp(-f64(og)))
    return y

@@ -1,0 +1,251 @@
+from contextlib import ExitStack
+
+import concourse.mybir as mybir
+
+H, D, NQ, N, E = 4, 128, 512, 512, 128
+FLOPS = 2 * H * N * NQ * D + 2 * H * NQ * N * E
+
+F32 = mybir.dt.float32
+BF16 = mybir.dt.bfloat16
+U32 = mybir.dt.uint32
+U8 = mybir.dt.uint8
+FP8X4 = mybir.dt.float8_e4m3fn_x4
+ALU = mybir.AluOpType
+ACT = mybir.ActivationFunctionType
+
+P = 128
+PACK = 4
+ROWS = 32
+TILE = 128
+RUN = 4
+
+
+def tile_rows_a_relu_kb_mask_gate_kernel(tc, qT, kT, t, v, kb, mask, og, out):
+    nc = tc.nc
+    with ExitStack() as ctx:
+        sb = ctx.enter_context(tc.tile_pool(name="sb", bufs=1))
+        ps = ctx.enter_context(tc.psum_pool(name="ps", bufs=1))
+        ctx.enter_context(tc.manual_schedule())
+
+        def sbuf(name, shape, dtype):
+            return sb.tile(shape, dtype, name=name, align_bytes=64)
+
+        k_raw = sbuf("k_raw", [P, PACK, N], F32)
+        k_bf = sbuf("k_bf", [P, PACK, TILE, PACK], BF16)
+        k_codes = sbuf("k_codes", [P, N], U32)
+        k_scales = sbuf("k_scales", [P, N], U8)
+        q_raw = [sbuf("q_raw%d" % c, [P, PACK, 256], F32) for c in range(2)]
+        q_bf = sbuf("q_bf", [P, 4, TILE, PACK], BF16)
+        q_codes = sbuf("q_codes", [P, NQ], U32)
+        q_scales = sbuf("q_scales", [P, NQ], U8)
+        v_raw = sbuf("v_raw", [P, PACK, E], F32)
+        v_bf = sbuf("v_bf", [P, E, PACK], BF16)
+        v_codes = sbuf("v_codes", [P, E], U32)
+        v_scales = sbuf("v_scales", [P, E], U8)
+        t_sb = sbuf("t_sb", [P, PACK], F32)
+        t_abs = sbuf("t_abs", [P, PACK], F32)
+        t_sign = sbuf("t_sign", [P, PACK], F32)
+        kb_sb = sbuf("kb_sb", [P, PACK], F32)
+        mask_raw = [sbuf("mask_raw%d" % r, [P, NQ], F32) for r in range(PACK)]
+        factor = [sbuf("factor%d" % r, [P, NQ], F32) for r in range(PACK)]
+        og_sb = [sbuf("og%d" % h, [P, 2, 2 * E], F32) for h in range(H)]
+        gate = [sbuf("gate%d" % h, [P, 2, 2 * E], F32) for h in range(H)]
+        x = [sbuf("x%d" % h, [P, PACK, NQ], BF16) for h in range(H)]
+        w_bf = [sbuf("w_bf%d" % h, [P, NQ, PACK], BF16) for h in range(H)]
+        w_codes = [sbuf("w_codes%d" % h, [P, NQ], U32) for h in range(H)]
+        w_scales = [sbuf("w_scales%d" % h, [P, NQ], U8) for h in range(H)]
+        res = [sbuf("res%d" % h, [P, 2, 2 * E], F32) for h in range(H)]
+
+        n_banks = [2, 1, 2, 2]
+        banks = [[ps.tile([P, NQ], F32, name="bank%d_%d" % (h, b)) for b in range(n_banks[h])] for h in range(H)]
+        y_bank = ps.tile([P, 4 * E], F32, name="y_bank")
+
+        def bank(h, r):
+            return banks[h][r % n_banks[h]]
+
+        og_v = [og[h].rearrange("(c m u) e -> m c (u e)", c=2, u=2) for h in range(H)]
+        out_v = [out[h].rearrange("(c m u) e -> m c (u e)", c=2, u=2) for h in range(H)]
+
+        nc.scalar.dma_start(out=og_sb[0][:, 0, 0:E], in_=og_v[0][:, 0, 0:E])
+        nc.scalar.dma_start(out=t_sb[:], in_=t.rearrange("(p r) o -> p (r o)", r=PACK))
+        nc.scalar.dma_start(out=kb_sb[:], in_=kb.rearrange("(p r) o -> p (r o)", r=PACK))
+        k_v = kT[0].rearrange("(p j) n -> p j n", j=PACK)
+        for g in (0, 2, 1, 3):
+            nc.sync.dma_start(out=k_raw[ROWS * g : ROWS * (g + 1)], in_=k_v)
+        q_v = qT.rearrange("h (p j) q -> (h p) j q", j=PACK)
+        for c in range(2):
+            nc.sync.dma_start(out=q_raw[c][:], in_=q_v[:, :, 256 * c : 256 * (c + 1)])
+        mask_v = mask.rearrange("(p r) q -> p r q", r=PACK)
+        for r in range(PACK):
+            nc.sync.dma_start(out=mask_raw[r][:], in_=mask_v[:, r, :])
+        nc.sync.dma_start(out=og_sb[0][:, 0, E : 2 * E], in_=og_v[0][:, 0, E : 2 * E])
+        nc.sync.dma_start(out=og_sb[0][:, 1, :], in_=og_v[0][:, 1, :])
+        nc.sync.dma_start(out=og_sb[1][:], in_=og_v[1])
+        nc.sync.dma_start(out=og_sb[2][:], in_=og_v[2])
+        nc.sync.dma_start(out=v_raw[:], in_=v[0].rearrange("(p j) e -> p j e", j=PACK))
+        nc.sync.dma_start(out=og_sb[3][:], in_=og_v[3])
+
+        def flat(ap3):
+            return ap3.rearrange("p a b -> p (a b)")
+
+        def quantise(codes, scales, cols, values):
+            nc.vector.quantize_mx(out=codes[:, cols].bitcast(FP8X4), scales=scales[:, cols], in_=values)
+
+        def sigmoid(h, lo, hi):
+            nc.scalar.activation(out=flat(gate[h][:])[:, lo:hi], in_=flat(og_sb[h][:])[:, lo:hi], func=ACT.Sigmoid)
+
+        def copy_on(engine, dst, src):
+            if engine == "vector":
+                nc.vector.tensor_copy(out=dst, in_=src)
+            else:
+                nc.scalar.copy(out=dst, in_=src)
+
+        def cast_k(engine, r0):
+            dst = k_bf[:, r0 : r0 + 2].rearrange("p r s j -> p s j r")
+            src = k_raw[:].rearrange("p j (s r) -> p s j r", r=PACK)[:, :, :, r0 : r0 + 2]
+            copy_on(engine, dst, src)
+
+        def quant_k(r0):
+            quantise(k_codes, k_scales, slice(TILE * r0, TILE * (r0 + 2)),
+                     k_bf[:, r0 : r0 + 2].rearrange("p r s j -> p (r s j)"))
+
+        def cast_q(engine, c, u):
+            dst = q_bf[:, 2 * c + u].rearrange("p (a i) j -> p a j i", i=RUN)
+            src = q_raw[c][:].rearrange("p j (a i u) -> p u a j i", i=RUN, u=2)[:, u]
+            copy_on(engine, dst, src)
+
+        def quant_q(c):
+            quantise(q_codes, q_scales, slice(256 * c, 256 * (c + 1)),
+                     q_bf[:, 2 * c : 2 * c + 2].rearrange("p a m j -> p (a m j)"))
+
+        def make_factor(r):
+            nc.scalar.activation(
+                out=factor[r][:].rearrange("p (c u m) -> p c u m", c=2, u=2),
+                in_=mask_raw[r][:].rearrange("p (c m u) -> p c u m", c=2, u=2),
+                func=ACT.Copy, scale=t_abs[:, r : r + 1])
+
+        def scores(h, r, tiles=(0, 1, 2, 3)):
+            rows = slice(ROWS * h, ROWS * (h + 1))
+            kc = slice(TILE * r, TILE * (r + 1))
+            for a in tiles:
+                qc = slice(TILE * a, TILE * (a + 1))
+                nc.tensor.matmul_mx(
+                    out=bank(h, r)[:, qc],
+                    lhsT=k_codes[rows, kc].bitcast(FP8X4), lhsT_scale=k_scales[rows, kc],
+                    rhs=q_codes[rows, qc].bitcast(FP8X4), rhs_scale=q_scales[rows, qc],
+                    start=True, stop=True)
+
+        def weigh(h, r):
+            nc.vector.scalar_tensor_tensor(
+                out=x[h][:, r, :], in0=bank(h, r)[:], scalar=kb_sb[:, r : r + 1], in1=factor[r][:],
+                op0=ALU.add, op1=ALU.mult)
+
+        def interleave(engine, h, lo, hi):
+            dst = w_bf[h][:, lo:hi, :].rearrange("p (a i) r -> p a r i", i=RUN)
+            src = x[h][:, :, lo:hi].rearrange("p r (a i) -> p a r i", i=RUN)
+            if engine == "vector":
+                nc.vector.tensor_scalar(out=dst, in0=src, scalar1=0.0, scalar2=None, op0=ALU.max)
+            else:
+                nc.scalar.activation(out=dst, in_=src, func=ACT.Relu)
+
+        def quant_w(h, lo, hi):
+            quantise(w_codes[h], w_scales[h], slice(lo, hi), flat(w_bf[h][:, lo:hi, :]))
+
+        def mix(h, tiles=(0, 1, 2, 3)):
+            for a in tiles:
+                qc = slice(TILE * a, TILE * (a + 1))
+                nc.tensor.matmul_mx(
+                    out=y_bank[:, E * a : E * (a + 1)],
+                    lhsT=w_codes[h][:, qc].bitcast(FP8X4), lhsT_scale=w_scales[h][:, qc],
+                    rhs=v_codes[:].bitcast(FP8X4), rhs_scale=v_scales[:],
+                    start=True, stop=True)
+
+        def finish(h, c0, c1):
+            nc.vector.scalar_tensor_tensor(
+                out=flat(res[h][:, c0:c1, :]), in0=y_bank[:, 2 * E * c0 : 2 * E * c1], scalar=1.0 / 16.0,
+                in1=flat(gate[h][:, c0:c1, :]), op0=ALU.mult, op1=ALU.mult)
+            nc.sync.dma_start(out=out_v[h][:, c0:c1, :], in_=res[h][:, c0:c1, :])
+
+        A, B, C, Z = 0, 1, 2, 3
+
+        sigmoid(A, 0, E)
+        nc.scalar.activation(out=t_abs[:], in_=t_sb[:], func=ACT.Abs)
+        nc.scalar.activation(out=t_sign[:], in_=t_sb[:], func=ACT.Sign)
+
+        cast_k("vector", 0)
+        cast_k("scalar", 2)
+        quant_k(0)
+        cast_q("vector", 0, 0)
+        cast_q("scalar", 0, 1)
+        quant_k(2)
+        quant_q(0)
+        scores(B, 0, (0, 1))
+        scores(A, 0, (0, 1))
+        scores(A, 1, (0, 1))
+        cast_q("vector", 1, 0)
+        cast_q("scalar", 1, 1)
+        quant_q(1)
+        scores(B, 0, (2, 3))
+        scores(A, 0, (2, 3))
+        scores(A, 1, (2, 3))
+        for r in range(PACK):
+            make_factor(r)
+        sigmoid(A, E, 4 * E)
+        sigmoid(B, 0, 4 * E)
+        sigmoid(C, 0, 4 * E)
+        nc.gpsimd.tensor_tensor(
+            out=v_bf[:], in0=v_raw[:].rearrange("p j e -> p e j"),
+            in1=t_sign[:].unsqueeze(1).to_broadcast([P, E, PACK]), op=ALU.mult)
+
+        weigh(B, 0)
+        scores(B, 1)
+        scores(C, 0)
+        weigh(A, 0)
+        scores(A, 2)
+        scores(Z, 0)
+        weigh(A, 1)
+        scores(A, 3)
+        scores(C, 1)
+        weigh(B, 1)
+        scores(B, 2)
+        scores(Z, 1)
+        weigh(A, 2)
+        weigh(A, 3)
+        interleave("scalar", A, 0, NQ)
+        weigh(B, 2)
+        scores(B, 3)
+        weigh(C, 0)
+        scores(C, 2)
+        weigh(C, 1)
+        scores(C, 3)
+        weigh(B, 3)
+        interleave("scalar", B, 0, NQ)
+        quantise(v_codes, v_scales, slice(0, E), flat(v_bf[:]))
+        quant_w(A, 0, NQ)
+        mix(A)
+        weigh(C, 2)
+        weigh(C, 3)
+        interleave("scalar", C, 0, NQ)
+        weigh(Z, 0)
+        scores(Z, 2)
+        finish(A, 0, 2)
+        weigh(Z, 1)
+        scores(Z, 3)
+        quant_w(B, 0, NQ)
+        mix(B)
+        weigh(Z, 2)
+        weigh(Z, 3)
+        interleave("scalar", Z, 128, 256)
+        interleave("scalar", Z, 256, NQ)
+        sigmoid(Z, 0, 4 * E)
+        finish(B, 0, 2)
+        quant_w(C, 0, NQ)
+        mix(C)
+        interleave("vector", Z, 0, 128)
+        quant_w(Z, 0, 256)
+        finish(C, 0, 2)
+        mix(Z, (0, 1))
+        quant_w(Z, 256, NQ)
+        mix(Z, (2, 3))
+        finish(Z, 0, 1)
+        finish(Z, 1, 2)

@@ -9,6 +9,7 @@ F32 = mybir.dt.float32
 BF16 = mybir.dt.bfloat16
 U32 = mybir.dt.uint32
 U8 = mybir.dt.uint8
+I32 = mybir.dt.int32
 FP8X4 = mybir.dt.float8_e4m3fn_x4
 ALU = mybir.AluOpType
 ACT = mybir.ActivationFunctionType
@@ -30,10 +31,12 @@ def tile_rows_a_relu_kb_mask_gate_kernel(tc, qT, kT, t, v, kb, mask, og, out):
         def sbuf(name, shape, dtype):
             return sb.tile(shape, dtype, name=name, align_bytes=64)
 
-        k_raw = sbuf("k_raw", [P, PACK, N], F32)
-        k_bf = sbuf("k_bf", [P, PACK, TILE, PACK], BF16)
-        k_codes = sbuf("k_codes", [P, N], U32)
-        k_scales = sbuf("k_scales", [P, N], U8)
+        k_raw = sbuf("k_raw", [ROWS, PACK, N], F32)
+        k_bf = sbuf("k_bf", [ROWS, PACK, TILE, PACK], BF16)
+        k_own = sbuf("k_own", [ROWS, N + N // 4], U32)
+        k_far = sbuf("k_far", [P, N + N // 4], U32)
+        k_codes = [(k_far if h else k_own)[:, 0:N] for h in range(H)]
+        k_scales = [(k_far if h else k_own)[:, N : N + N // 4].bitcast(U8) for h in range(H)]
         q_raw = [sbuf("q_raw%d" % c, [P, PACK, 256], F32) for c in range(2)]
         q_bf = sbuf("q_bf", [P, 4, TILE, PACK], BF16)
         q_codes = sbuf("q_codes", [P, NQ], U32)
@@ -56,7 +59,7 @@ def tile_rows_a_relu_kb_mask_gate_kernel(tc, qT, kT, t, v, kb, mask, og, out):
         w_scales = [sbuf("w_scales%d" % h, [P, NQ], U8) for h in range(H)]
         res = [sbuf("res%d" % h, [P, 2, 2 * E], F32) for h in range(H)]
 
-        n_banks = [2, 1, 2, 2]
+        n_banks = [2, 2, 1, 2]
         banks = [[ps.tile([P, NQ], F32, name="bank%d_%d" % (h, b)) for b in range(n_banks[h])] for h in range(H)]
         y_bank = ps.tile([P, 4 * E], F32, name="y_bank")
 
@@ -67,23 +70,15 @@ def tile_rows_a_relu_kb_mask_gate_kernel(tc, qT, kT, t, v, kb, mask, og, out):
         out_v = [out[h].rearrange("(c m u) e -> m c (u e)", c=2, u=2) for h in range(H)]
 
         nc.scalar.dma_start(out=og_sb[0][:, 0, 0:E], in_=og_v[0][:, 0, 0:E])
-        nc.scalar.dma_start(out=t_sb[:], in_=t.rearrange("(p r) o -> p (r o)", r=PACK))
-        nc.scalar.dma_start(out=kb_sb[:], in_=kb.rearrange("(p r) o -> p (r o)", r=PACK))
-        k_v = kT[0].rearrange("(p j) n -> p j n", j=PACK)
-        for g in (0, 2, 1, 3):
-            nc.sync.dma_start(out=k_raw[ROWS * g : ROWS * (g + 1)], in_=k_v)
+        nc.gpsimd.dma_start(out=t_sb[:], in_=t.rearrange("(p r) o -> p (r o)", r=PACK))
+        nc.gpsimd.dma_start(out=kb_sb[:], in_=kb.rearrange("(p r) o -> p (r o)", r=PACK))
+        nc.sync.dma_start(out=k_raw[:], in_=kT[0].rearrange("(p j) n -> p j n", j=PACK))
         q_v = qT.rearrange("h (p j) q -> (h p) j q", j=PACK)
         for c in range(2):
             nc.sync.dma_start(out=q_raw[c][:], in_=q_v[:, :, 256 * c : 256 * (c + 1)])
         mask_v = mask.rearrange("(p r) q -> p r q", r=PACK)
-        for r in range(PACK):
-            nc.sync.dma_start(out=mask_raw[r][:], in_=mask_v[:, r, :])
-        nc.sync.dma_start(out=og_sb[0][:, 0, E : 2 * E], in_=og_v[0][:, 0, E : 2 * E])
-        nc.sync.dma_start(out=og_sb[0][:, 1, :], in_=og_v[0][:, 1, :])
-        nc.sync.dma_start(out=og_sb[1][:], in_=og_v[1])
-        nc.sync.dma_start(out=og_sb[2][:], in_=og_v[2])
-        nc.sync.dma_start(out=v_raw[:], in_=v[0].rearrange("(p j) e -> p j e", j=PACK))
-        nc.sync.dma_start(out=og_sb[3][:], in_=og_v[3])
+        nc.sync.dma_start(out=mask_raw[0][:], in_=mask_v[:, 0, :])
+        nc.sync.dma_start(out=mask_raw[1][:], in_=mask_v[:, 1, :])
 
         def flat(ap3):
             return ap3.rearrange("p a b -> p (a b)")
@@ -100,18 +95,14 @@ def tile_rows_a_relu_kb_mask_gate_kernel(tc, qT, kT, t, v, kb, mask, og, out):
             else:
                 nc.scalar.copy(out=dst, in_=src)
 
-        def cast_k(engine, r0):
-            dst = k_bf[:, r0 : r0 + 2].rearrange("p r s j -> p s j r")
-            src = k_raw[:].rearrange("p j (s r) -> p s j r", r=PACK)[:, :, :, r0 : r0 + 2]
+        def cast_k(engine, r0, lo, hi):
+            dst = k_bf[:, r0 : r0 + 2, lo:hi].rearrange("p r s j -> p s j r")
+            src = k_raw[:].rearrange("p j (s r) -> p s j r", r=PACK)[:, lo:hi, :, r0 : r0 + 2]
             copy_on(engine, dst, src)
 
-        def quant_k(r0):
-            quantise(k_codes, k_scales, slice(TILE * r0, TILE * (r0 + 2)),
-                     k_bf[:, r0 : r0 + 2].rearrange("p r s j -> p (r s j)"))
-
-        def cast_q(engine, c, u):
-            dst = q_bf[:, 2 * c + u].rearrange("p (a i) j -> p a j i", i=RUN)
-            src = q_raw[c][:].rearrange("p j (a i u) -> p u a j i", i=RUN, u=2)[:, u]
+        def cast_q(engine, c, u, lo=0, hi=TILE // RUN):
+            dst = q_bf[:, 2 * c + u].rearrange("p (a i) j -> p a j i", i=RUN)[:, lo:hi]
+            src = q_raw[c][:].rearrange("p j (a i u) -> p u a j i", i=RUN, u=2)[:, u, lo:hi]
             copy_on(engine, dst, src)
 
         def quant_q(c):
@@ -131,7 +122,7 @@ def tile_rows_a_relu_kb_mask_gate_kernel(tc, qT, kT, t, v, kb, mask, og, out):
                 qc = slice(TILE * a, TILE * (a + 1))
                 nc.tensor.matmul_mx(
                     out=bank(h, r)[:, qc],
-                    lhsT=k_codes[rows, kc].bitcast(FP8X4), lhsT_scale=k_scales[rows, kc],
+                    lhsT=k_codes[h][rows, kc].bitcast(FP8X4), lhsT_scale=k_scales[h][rows, kc],
                     rhs=q_codes[rows, qc].bitcast(FP8X4), rhs_scale=q_scales[rows, qc],
                     start=True, stop=True)
 
@@ -168,62 +159,77 @@ def tile_rows_a_relu_kb_mask_gate_kernel(tc, qT, kT, t, v, kb, mask, og, out):
 
         A, B, C, Z = 0, 1, 2, 3
 
+        nc.vector.memset(k_own[:, N : N + N // 4], 0)
         sigmoid(A, 0, E)
-        nc.scalar.activation(out=t_abs[:], in_=t_sb[:], func=ACT.Abs)
-        nc.scalar.activation(out=t_sign[:], in_=t_sb[:], func=ACT.Sign)
 
-        cast_k("vector", 0)
-        cast_k("scalar", 2)
-        quant_k(0)
+        cast_k("scalar", 2, 40, TILE)
+        cast_k("vector", 0, 0, TILE)
+        cast_k("vector", 2, 0, 40)
+        nc.vector.quantize_mx(out=k_codes[0].bitcast(FP8X4), scales=k_scales[0],
+                              in_=k_bf[:].rearrange("p r s j -> p (r s j)"))
         cast_q("vector", 0, 0)
         cast_q("scalar", 0, 1)
-        quant_k(2)
+        for g in (C, B, Z):
+            nc.scalar.dma_start(out=k_far[ROWS * g : ROWS * (g + 1), :].bitcast(I32), in_=k_own[:].bitcast(I32))
+        nc.sync.dma_start(out=og_sb[0][:, 0, E : 2 * E], in_=og_v[0][:, 0, E : 2 * E])
+        nc.sync.dma_start(out=og_sb[0][:, 1, :], in_=og_v[0][:, 1, :])
+        nc.sync.dma_start(out=mask_raw[2][:], in_=mask_v[:, 2, :])
+        nc.sync.dma_start(out=og_sb[1][:], in_=og_v[1])
+        nc.sync.dma_start(out=mask_raw[3][:], in_=mask_v[:, 3, :])
+        nc.sync.dma_start(out=og_sb[2][:], in_=og_v[2])
+        nc.sync.dma_start(out=v_raw[:], in_=v[0].rearrange("(p j) e -> p j e", j=PACK))
+        nc.sync.dma_start(out=og_sb[3][:], in_=og_v[3])
+        nc.scalar.activation(out=t_abs[:], in_=t_sb[:], func=ACT.Abs)
+        nc.scalar.activation(out=t_sign[:], in_=t_sb[:], func=ACT.Sign)
         quant_q(0)
-        scores(B, 0, (0, 1))
         scores(A, 0, (0, 1))
         scores(A, 1, (0, 1))
+        cast_q("scalar", 1, 1, 10)
         cast_q("vector", 1, 0)
-        cast_q("scalar", 1, 1)
+        cast_q("vector", 1, 1, 0, 10)
         quant_q(1)
-        scores(B, 0, (2, 3))
         scores(A, 0, (2, 3))
         scores(A, 1, (2, 3))
-        for r in range(PACK):
-            make_factor(r)
+        scores(C, 0)
+        make_factor(0)
+        make_factor(1)
         sigmoid(A, E, 4 * E)
+        make_factor(2)
         sigmoid(B, 0, 4 * E)
+        make_factor(3)
         sigmoid(C, 0, 4 * E)
         nc.gpsimd.tensor_tensor(
             out=v_bf[:], in0=v_raw[:].rearrange("p j e -> p e j"),
             in1=t_sign[:].unsqueeze(1).to_broadcast([P, E, PACK]), op=ALU.mult)
 
-        weigh(B, 0)
-        scores(B, 1)
-        scores(C, 0)
         weigh(A, 0)
         scores(A, 2)
-        scores(Z, 0)
         weigh(A, 1)
         scores(A, 3)
+        scores(B, 0)
+        weigh(C, 0)
         scores(C, 1)
-        weigh(B, 1)
-        scores(B, 2)
-        scores(Z, 1)
+        scores(B, 1)
         weigh(A, 2)
         weigh(A, 3)
         interleave("scalar", A, 0, NQ)
-        weigh(B, 2)
-        scores(B, 3)
-        weigh(C, 0)
-        scores(C, 2)
+        sigmoid(Z, 0, 4 * E)
+        weigh(B, 0)
+        scores(B, 2)
         weigh(C, 1)
+        scores(C, 2)
+        weigh(B, 1)
+        scores(B, 3)
+        scores(Z, 0)
+        weigh(B, 2)
+        weigh(C, 2)
         scores(C, 3)
+        scores(Z, 1)
         weigh(B, 3)
         interleave("scalar", B, 0, NQ)
         quantise(v_codes, v_scales, slice(0, E), flat(v_bf[:]))
         quant_w(A, 0, NQ)
         mix(A)
-        weigh(C, 2)
         weigh(C, 3)
         interleave("scalar", C, 0, NQ)
         weigh(Z, 0)
@@ -237,7 +243,6 @@ def tile_rows_a_relu_kb_mask_gate_kernel(tc, qT, kT, t, v, kb, mask, og, out):
         weigh(Z, 3)
         interleave("scalar", Z, 128, 256)
         interleave("scalar", Z, 256, NQ)
-        sigmoid(Z, 0, 4 * E)
         finish(B, 0, 2)
         quant_w(C, 0, NQ)
         mix(C)

@@ -50,7 +50,7 @@ def tile_rows_a_relu_kb_mask_gate_kernel(tc, qT, kT, t, v, kb, mask, og, out):
         t_sign = sbuf("t_sign", [P, PACK], F32)
         kb_sb = sbuf("kb_sb", [P, PACK], F32)
         mask_raw = [sbuf("mask_raw%d" % r, [P, NQ], F32) for r in range(PACK)]
-        factor = [sbuf("factor%d" % r, [P, NQ], F32) for r in range(PACK)]
+        factor = sbuf("factor", [P, PACK, NQ], F32)
         og_sb = [sbuf("og%d" % h, [P, 2, 2 * E], F32) for h in range(H)]
         gate = [sbuf("gate%d" % h, [P, 2, 2 * E], F32) for h in range(H)]
         x = [sbuf("x%d" % h, [P, PACK, NQ], BF16) for h in range(H)]
@@ -109,11 +109,17 @@ def tile_rows_a_relu_kb_mask_gate_kernel(tc, qT, kT, t, v, kb, mask, og, out):
             quantise(q_codes, q_scales, slice(256 * c, 256 * (c + 1)),
                      q_bf[:, 2 * c : 2 * c + 2].rearrange("p a m j -> p (a m j)"))
 
-        def make_factor(r):
-            nc.scalar.activation(
-                out=factor[r][:].rearrange("p (c u m) -> p c u m", c=2, u=2),
-                in_=mask_raw[r][:].rearrange("p (c m u) -> p c u m", c=2, u=2),
-                func=ACT.Copy, scale=t_abs[:, r : r + 1])
+        def quant_qt(a):
+            quantise(q_codes, q_scales, slice(TILE * a, TILE * (a + 1)), flat(q_bf[:, a]))
+
+        def make_factor(engine, r):
+            dst = factor[:, r, :].rearrange("p (c u m) -> p c u m", c=2, u=2)
+            src = mask_raw[r][:].rearrange("p (c m u) -> p c u m", c=2, u=2)
+            if engine == "scalar":
+                nc.scalar.activation(out=dst, in_=src, func=ACT.Copy, scale=t_abs[:, r : r + 1])
+            else:
+                nc.gpsimd.tensor_scalar(out=dst, in0=src, scalar1=t_abs[:, r : r + 1], scalar2=0.0,
+                                        op0=ALU.mult, op1=ALU.add)
 
         def scores(h, r, tiles=(0, 1, 2, 3)):
             rows = slice(ROWS * h, ROWS * (h + 1))
@@ -128,7 +134,7 @@ def tile_rows_a_relu_kb_mask_gate_kernel(tc, qT, kT, t, v, kb, mask, og, out):
 
         def weigh(h, r):
             nc.vector.scalar_tensor_tensor(
-                out=x[h][:, r, :], in0=bank(h, r)[:], scalar=kb_sb[:, r : r + 1], in1=factor[r][:],
+                out=x[h][:, r, :], in0=bank(h, r)[:], scalar=kb_sb[:, r : r + 1], in1=factor[:, r, :],
                 op0=ALU.add, op1=ALU.mult)
 
         def interleave(engine, h, lo, hi):
@@ -167,17 +173,21 @@ def tile_rows_a_relu_kb_mask_gate_kernel(tc, qT, kT, t, v, kb, mask, og, out):
         cast_k("vector", 2, 0, 40)
         nc.vector.quantize_mx(out=k_codes[0].bitcast(FP8X4), scales=k_scales[0],
                               in_=k_bf[:].rearrange("p r s j -> p (r s j)"))
+        for g in (C,):
+            nc.sync.dma_start(out=k_far[ROWS * g : ROWS * (g + 1), :].bitcast(I32), in_=k_own[:].bitcast(I32))
         cast_q("vector", 0, 0)
         cast_q("scalar", 0, 1)
-        for g in (C, B, Z):
-            nc.scalar.dma_start(out=k_far[ROWS * g : ROWS * (g + 1), :].bitcast(I32), in_=k_own[:].bitcast(I32))
+        nc.sync.dma_start(out=mask_raw[2][:], in_=mask_v[:, 2, :])
+        nc.sync.dma_start(out=mask_raw[3][:], in_=mask_v[:, 3, :])
+        for g in (B,):
+            nc.sync.dma_start(out=k_far[ROWS * g : ROWS * (g + 1), :].bitcast(I32), in_=k_own[:].bitcast(I32))
         nc.sync.dma_start(out=og_sb[0][:, 0, E : 2 * E], in_=og_v[0][:, 0, E : 2 * E])
         nc.sync.dma_start(out=og_sb[0][:, 1, :], in_=og_v[0][:, 1, :])
-        nc.sync.dma_start(out=mask_raw[2][:], in_=mask_v[:, 2, :])
         nc.sync.dma_start(out=og_sb[1][:], in_=og_v[1])
-        nc.sync.dma_start(out=mask_raw[3][:], in_=mask_v[:, 3, :])
-        nc.sync.dma_start(out=og_sb[2][:], in_=og_v[2])
+        for g in (Z,):
+            nc.sync.dma_start(out=k_far[ROWS * g : ROWS * (g + 1), :].bitcast(I32), in_=k_own[:].bitcast(I32))
         nc.sync.dma_start(out=v_raw[:], in_=v[0].rearrange("(p j) e -> p j e", j=PACK))
+        nc.sync.dma_start(out=og_sb[2][:], in_=og_v[2])
         nc.sync.dma_start(out=og_sb[3][:], in_=og_v[3])
         nc.scalar.activation(out=t_abs[:], in_=t_sb[:], func=ACT.Abs)
         nc.scalar.activation(out=t_sign[:], in_=t_sb[:], func=ACT.Sign)
@@ -187,21 +197,21 @@ def tile_rows_a_relu_kb_mask_gate_kernel(tc, qT, kT, t, v, kb, mask, og, out):
         cast_q("scalar", 1, 1, 10)
         cast_q("vector", 1, 0)
         cast_q("vector", 1, 1, 0, 10)
-        quant_q(1)
-        scores(A, 0, (2, 3))
+        quant_qt(2)
+        scores(A, 0, (2,))
+        quant_qt(3)
+        scores(A, 0, (3,))
         scores(A, 1, (2, 3))
         scores(C, 0)
-        make_factor(0)
-        make_factor(1)
+        make_factor("scalar", 0)
+        make_factor("scalar", 1)
+        make_factor("scalar", 2)
+        make_factor("scalar", 3)
         sigmoid(A, E, 4 * E)
-        make_factor(2)
         sigmoid(B, 0, 4 * E)
-        make_factor(3)
-        sigmoid(C, 0, 4 * E)
         nc.gpsimd.tensor_tensor(
             out=v_bf[:], in0=v_raw[:].rearrange("p j e -> p e j"),
             in1=t_sign[:].unsqueeze(1).to_broadcast([P, E, PACK]), op=ALU.mult)
-
         weigh(A, 0)
         scores(A, 2)
         weigh(A, 1)
@@ -212,8 +222,8 @@ def tile_rows_a_relu_kb_mask_gate_kernel(tc, qT, kT, t, v, kb, mask, og, out):
         scores(B, 1)
         weigh(A, 2)
         weigh(A, 3)
-        interleave("scalar", A, 0, NQ)
-        sigmoid(Z, 0, 4 * E)
+        interleave("scalar", A, 0, 512)
+        sigmoid(C, 0, 4 * E)
         weigh(B, 0)
         scores(B, 2)
         weigh(C, 1)
@@ -226,31 +236,32 @@ def tile_rows_a_relu_kb_mask_gate_kernel(tc, qT, kT, t, v, kb, mask, og, out):
         scores(C, 3)
         scores(Z, 1)
         weigh(B, 3)
-        interleave("scalar", B, 0, NQ)
+        interleave("scalar", B, 0, 512)
         quantise(v_codes, v_scales, slice(0, E), flat(v_bf[:]))
-        quant_w(A, 0, NQ)
+        quant_w(A, 0, 512)
         mix(A)
         weigh(C, 3)
-        interleave("scalar", C, 0, NQ)
+        interleave("scalar", C, 0, 512)
         weigh(Z, 0)
         scores(Z, 2)
         finish(A, 0, 2)
         weigh(Z, 1)
         scores(Z, 3)
-        quant_w(B, 0, NQ)
+        quant_w(B, 0, 512)
         mix(B)
         weigh(Z, 2)
         weigh(Z, 3)
         interleave("scalar", Z, 128, 256)
-        interleave("scalar", Z, 256, NQ)
+        interleave("scalar", Z, 256, 512)
+        sigmoid(Z, 0, 4 * E)
         finish(B, 0, 2)
-        quant_w(C, 0, NQ)
+        quant_w(C, 0, 512)
         mix(C)
         interleave("vector", Z, 0, 128)
         quant_w(Z, 0, 256)
         finish(C, 0, 2)
         mix(Z, (0, 1))
-        quant_w(Z, 256, NQ)
+        quant_w(Z, 256, 512)
         mix(Z, (2, 3))
         finish(Z, 0, 1)
         finish(Z, 1, 2)

from contextlib import ExitStack

import concourse.mybir as mybir

H, D, NQ, N, E = 4, 128, 512, 512, 128
FLOPS = 2 * H * N * NQ * D + 2 * H * NQ * N * E

F32 = mybir.dt.float32
BF16 = mybir.dt.bfloat16
U32 = mybir.dt.uint32
U8 = mybir.dt.uint8
I32 = mybir.dt.int32
FP8X4 = mybir.dt.float8_e4m3fn_x4
ALU = mybir.AluOpType
ACT = mybir.ActivationFunctionType

P = 128
PACK = 4
ROWS = 32
TILE = 128
RUN = 4


def tile_rows_a_relu_kb_mask_gate_kernel(tc, qT, kT, t, v, kb, mask, og, out):
    nc = tc.nc
    with ExitStack() as ctx:
        sb = ctx.enter_context(tc.tile_pool(name="sb", bufs=1))
        ps = ctx.enter_context(tc.psum_pool(name="ps", bufs=1))
        ctx.enter_context(tc.manual_schedule())

        def sbuf(name, shape, dtype):
            return sb.tile(shape, dtype, name=name, align_bytes=64)

        k_raw = sbuf("k_raw", [ROWS, PACK, N], F32)
        k_bf = sbuf("k_bf", [ROWS, PACK, TILE, PACK], BF16)
        k_own = sbuf("k_own", [ROWS, N + N // 4], U32)
        k_far = sbuf("k_far", [P, N + N // 4], U32)
        k_codes = [(k_far if h else k_own)[:, 0:N] for h in range(H)]
        k_scales = [(k_far if h else k_own)[:, N : N + N // 4].bitcast(U8) for h in range(H)]
        q_raw = [sbuf("q_raw%d" % c, [P, PACK, 256], F32) for c in range(2)]
        q_bf = sbuf("q_bf", [P, 4, TILE, PACK], BF16)
        q_codes = sbuf("q_codes", [P, NQ], U32)
        q_scales = sbuf("q_scales", [P, NQ], U8)
        v_raw = sbuf("v_raw", [P, PACK, E], F32)
        v_bf = sbuf("v_bf", [P, E, PACK], BF16)
        v_codes = sbuf("v_codes", [P, E], U32)
        v_scales = sbuf("v_scales", [P, E], U8)
        t_sb = sbuf("t_sb", [P, PACK], F32)
        t_abs = sbuf("t_abs", [P, PACK], F32)
        t_sign = sbuf("t_sign", [P, PACK], F32)
        kb_sb = sbuf("kb_sb", [P, PACK], F32)
        mask_raw = [sbuf("mask_raw%d" % r, [P, NQ], F32) for r in range(PACK)]
        factor = sbuf("factor", [P, PACK, NQ], F32)
        og_sb = [sbuf("og%d" % h, [P, 2, 2 * E], F32) for h in range(H)]
        gate = [sbuf("gate%d" % h, [P, 2, 2 * E], F32) for h in range(H)]
        x = [sbuf("x%d" % h, [P, PACK, NQ], BF16) for h in range(H)]
        w_bf = [sbuf("w_bf%d" % h, [P, NQ, PACK], BF16) for h in range(H)]
        w_codes = [sbuf("w_codes%d" % h, [P, NQ], U32) for h in range(H)]
        w_scales = [sbuf("w_scales%d" % h, [P, NQ], U8) for h in range(H)]
        res = [sbuf("res%d" % h, [P, 2, 2 * E], F32) for h in range(H)]

        n_banks = [2, 2, 1, 2]
        banks = [[ps.tile([P, NQ], F32, name="bank%d_%d" % (h, b)) for b in range(n_banks[h])] for h in range(H)]
        y_bank = ps.tile([P, 4 * E], F32, name="y_bank")

        def bank(h, r):
            return banks[h][r % n_banks[h]]

        og_v = [og[h].rearrange("(c m u) e -> m c (u e)", c=2, u=2) for h in range(H)]
        out_v = [out[h].rearrange("(c m u) e -> m c (u e)", c=2, u=2) for h in range(H)]

        nc.scalar.dma_start(out=og_sb[0][:, 0, 0:E], in_=og_v[0][:, 0, 0:E])
        nc.gpsimd.dma_start(out=t_sb[:], in_=t.rearrange("(p r) o -> p (r o)", r=PACK))
        nc.gpsimd.dma_start(out=kb_sb[:], in_=kb.rearrange("(p r) o -> p (r o)", r=PACK))
        nc.sync.dma_start(out=k_raw[:], in_=kT[0].rearrange("(p j) n -> p j n", j=PACK))
        q_v = qT.rearrange("h (p j) q -> (h p) j q", j=PACK)
        for c in range(2):
            nc.sync.dma_start(out=q_raw[c][:], in_=q_v[:, :, 256 * c : 256 * (c + 1)])
        mask_v = mask.rearrange("(p r) q -> p r q", r=PACK)
        nc.sync.dma_start(out=mask_raw[0][:], in_=mask_v[:, 0, :])
        nc.sync.dma_start(out=mask_raw[1][:], in_=mask_v[:, 1, :])

        def flat(ap3):
            return ap3.rearrange("p a b -> p (a b)")

        def quantise(codes, scales, cols, values):
            nc.vector.quantize_mx(out=codes[:, cols].bitcast(FP8X4), scales=scales[:, cols], in_=values)

        def sigmoid(h, lo, hi):
            nc.scalar.activation(out=flat(gate[h][:])[:, lo:hi], in_=flat(og_sb[h][:])[:, lo:hi], func=ACT.Sigmoid)

        def copy_on(engine, dst, src):
            if engine == "vector":
                nc.vector.tensor_copy(out=dst, in_=src)
            else:
                nc.scalar.copy(out=dst, in_=src)

        def cast_k(engine, r0, lo, hi):
            dst = k_bf[:, r0 : r0 + 2, lo:hi].rearrange("p r s j -> p s j r")
            src = k_raw[:].rearrange("p j (s r) -> p s j r", r=PACK)[:, lo:hi, :, r0 : r0 + 2]
            copy_on(engine, dst, src)

        def cast_q(engine, c, u, lo=0, hi=TILE // RUN):
            dst = q_bf[:, 2 * c + u].rearrange("p (a i) j -> p a j i", i=RUN)[:, lo:hi]
            src = q_raw[c][:].rearrange("p j (a i u) -> p u a j i", i=RUN, u=2)[:, u, lo:hi]
            copy_on(engine, dst, src)

        def quant_q(c):
            quantise(q_codes, q_scales, slice(256 * c, 256 * (c + 1)),
                     q_bf[:, 2 * c : 2 * c + 2].rearrange("p a m j -> p (a m j)"))

        def quant_qt(a):
            quantise(q_codes, q_scales, slice(TILE * a, TILE * (a + 1)), flat(q_bf[:, a]))

        def make_factor(engine, r):
            dst = factor[:, r, :].rearrange("p (c u m) -> p c u m", c=2, u=2)
            src = mask_raw[r][:].rearrange("p (c m u) -> p c u m", c=2, u=2)
            if engine == "scalar":
                nc.scalar.activation(out=dst, in_=src, func=ACT.Copy, scale=t_abs[:, r : r + 1])
            else:
                nc.gpsimd.tensor_scalar(out=dst, in0=src, scalar1=t_abs[:, r : r + 1], scalar2=0.0,
                                        op0=ALU.mult, op1=ALU.add)

        def scores(h, r, tiles=(0, 1, 2, 3)):
            rows = slice(ROWS * h, ROWS * (h + 1))
            kc = slice(TILE * r, TILE * (r + 1))
            for a in tiles:
                qc = slice(TILE * a, TILE * (a + 1))
                nc.tensor.matmul_mx(
                    out=bank(h, r)[:, qc],
                    lhsT=k_codes[h][rows, kc].bitcast(FP8X4), lhsT_scale=k_scales[h][rows, kc],
                    rhs=q_codes[rows, qc].bitcast(FP8X4), rhs_scale=q_scales[rows, qc],
                    start=True, stop=True)

        def weigh(h, r):
            nc.vector.scalar_tensor_tensor(
                out=x[h][:, r, :], in0=bank(h, r)[:], scalar=kb_sb[:, r : r + 1], in1=factor[:, r, :],
                op0=ALU.add, op1=ALU.mult)

        def interleave(engine, h, lo, hi):
            dst = w_bf[h][:, lo:hi, :].rearrange("p (a i) r -> p a r i", i=RUN)
            src = x[h][:, :, lo:hi].rearrange("p r (a i) -> p a r i", i=RUN)
            if engine == "vector":
                nc.vector.tensor_scalar(out=dst, in0=src, scalar1=0.0, scalar2=None, op0=ALU.max)
            else:
                nc.scalar.activation(out=dst, in_=src, func=ACT.Relu)

        def quant_w(h, lo, hi):
            quantise(w_codes[h], w_scales[h], slice(lo, hi), flat(w_bf[h][:, lo:hi, :]))

        def mix(h, tiles=(0, 1, 2, 3)):
            for a in tiles:
                qc = slice(TILE * a, TILE * (a + 1))
                nc.tensor.matmul_mx(
                    out=y_bank[:, E * a : E * (a + 1)],
                    lhsT=w_codes[h][:, qc].bitcast(FP8X4), lhsT_scale=w_scales[h][:, qc],
                    rhs=v_codes[:].bitcast(FP8X4), rhs_scale=v_scales[:],
                    start=True, stop=True)

        def finish(h, c0, c1):
            nc.vector.scalar_tensor_tensor(
                out=flat(res[h][:, c0:c1, :]), in0=y_bank[:, 2 * E * c0 : 2 * E * c1], scalar=1.0 / 16.0,
                in1=flat(gate[h][:, c0:c1, :]), op0=ALU.mult, op1=ALU.mult)
            nc.sync.dma_start(out=out_v[h][:, c0:c1, :], in_=res[h][:, c0:c1, :])

        A, B, C, Z = 0, 1, 2, 3

        nc.vector.memset(k_own[:, N : N + N // 4], 0)
        sigmoid(A, 0, E)

        cast_k("scalar", 2, 40, TILE)
        cast_k("vector", 0, 0, TILE)
        cast_k("vector", 2, 0, 40)
        nc.vector.quantize_mx(out=k_codes[0].bitcast(FP8X4), scales=k_scales[0],
                              in_=k_bf[:].rearrange("p r s j -> p (r s j)"))
        for g in (C,):
            nc.sync.dma_start(out=k_far[ROWS * g : ROWS * (g + 1), :].bitcast(I32), in_=k_own[:].bitcast(I32))
        cast_q("vector", 0, 0)
        cast_q("scalar", 0, 1)
        nc.sync.dma_start(out=mask_raw[2][:], in_=mask_v[:, 2, :])
        nc.sync.dma_start(out=mask_raw[3][:], in_=mask_v[:, 3, :])
        for g in (B,):
            nc.sync.dma_start(out=k_far[ROWS * g : ROWS * (g + 1), :].bitcast(I32), in_=k_own[:].bitcast(I32))
        nc.sync.dma_start(out=og_sb[0][:, 0, E : 2 * E], in_=og_v[0][:, 0, E : 2 * E])
        nc.sync.dma_start(out=og_sb[0][:, 1, :], in_=og_v[0][:, 1, :])
        nc.sync.dma_start(out=og_sb[1][:], in_=og_v[1])
        for g in (Z,):
            nc.sync.dma_start(out=k_far[ROWS * g : ROWS * (g + 1), :].bitcast(I32), in_=k_own[:].bitcast(I32))
        nc.sync.dma_start(out=v_raw[:], in_=v[0].rearrange("(p j) e -> p j e", j=PACK))
        nc.sync.dma_start(out=og_sb[2][:], in_=og_v[2])
        nc.sync.dma_start(out=og_sb[3][:], in_=og_v[3])
        nc.scalar.activation(out=t_abs[:], in_=t_sb[:], func=ACT.Abs)
        nc.scalar.activation(out=t_sign[:], in_=t_sb[:], func=ACT.Sign)
        quant_q(0)
        scores(A, 0, (0, 1))
        scores(A, 1, (0, 1))
        cast_q("scalar", 1, 1, 10)
        cast_q("vector", 1, 0)
        cast_q("vector", 1, 1, 0, 10)
        quant_qt(2)
        scores(A, 0, (2,))
        quant_qt(3)
        scores(A, 0, (3,))
        scores(A, 1, (2, 3))
        scores(C, 0)
        make_factor("scalar", 0)
        make_factor("scalar", 1)
        make_factor("scalar", 2)
        make_factor("scalar", 3)
        sigmoid(A, E, 4 * E)
        sigmoid(B, 0, 4 * E)
        nc.gpsimd.tensor_tensor(
            out=v_bf[:], in0=v_raw[:].rearrange("p j e -> p e j"),
            in1=t_sign[:].unsqueeze(1).to_broadcast([P, E, PACK]), op=ALU.mult)
        weigh(A, 0)
        scores(A, 2)
        weigh(A, 1)
        scores(A, 3)
        scores(B, 0)
        weigh(C, 0)
        scores(C, 1)
        scores(B, 1)
        weigh(A, 2)
        weigh(A, 3)
        interleave("scalar", A, 0, 512)
        sigmoid(C, 0, 4 * E)
        weigh(B, 0)
        scores(B, 2)
        weigh(C, 1)
        scores(C, 2)
        weigh(B, 1)
        scores(B, 3)
        scores(Z, 0)
        weigh(B, 2)
        weigh(C, 2)
        scores(C, 3)
        scores(Z, 1)
        weigh(B, 3)
        interleave("scalar", B, 0, 512)
        quantise(v_codes, v_scales, slice(0, E), flat(v_bf[:]))
        quant_w(A, 0, 512)
        mix(A)
        weigh(C, 3)
        interleave("scalar", C, 0, 512)
        weigh(Z, 0)
        scores(Z, 2)
        finish(A, 0, 2)
        weigh(Z, 1)
        scores(Z, 3)
        quant_w(B, 0, 512)
        mix(B)
        weigh(Z, 2)
        weigh(Z, 3)
        interleave("scalar", Z, 128, 256)
        interleave("scalar", Z, 256, 512)
        sigmoid(Z, 0, 4 * E)
        finish(B, 0, 2)
        quant_w(C, 0, 512)
        mix(C)
        interleave("vector", Z, 0, 128)
        quant_w(Z, 0, 256)
        finish(C, 0, 2)
        mix(Z, (0, 1))
        quant_w(Z, 256, 512)
        mix(Z, (2, 3))
        finish(Z, 0, 1)
        finish(Z, 1, 2)
